import numpy as np
import ml_dtypes


def mxq(x, axis, fmt="e4m3"):
    dtype, down = {"e4m3": (ml_dtypes.float8_e4m3fn, 7), "e5m2": (ml_dtypes.float8_e5m2, 14)}[fmt]
    v = np.moveaxis(np.asarray(x, np.float32).astype(ml_dtypes.bfloat16).astype(np.float64), axis, -1)
    blocks = v.reshape(v.shape[:-1] + (-1, 32))
    amax = np.abs(blocks).max(-1, keepdims=True)
    byte = np.maximum(np.where(amax > 0, np.frexp(amax)[1] - 1 + 127, 0) - down, 1)
    scale = np.exp2(byte - 127.0)
    codes = (blocks / scale).astype(np.float32).astype(dtype).astype(np.float64)
    return np.moveaxis((codes * scale).reshape(v.shape), -1, axis)


WIDE = False


def mx_kscale(k):
    if not WIDE:
        return np.ones(k)
    levels = np.array([30, -30])
    if k % 512:
        return np.exp2(np.random.permutation(np.resize(levels, k // 32))).repeat(32)
    a = np.empty((k // 512, 16))
    for p in range(k // 512):
        a[p, :8] = np.random.permutation(np.resize(levels, 8))
        for g in range(8):
            far = levels[np.abs(levels - a[p, g]) >= 10]
            a[p, g + 8] = far[np.random.randint(len(far))]
    return np.exp2(a.ravel()).repeat(32)


def f64(x):
    return np.asarray(x).astype(np.float64)


def striped(idx):
    return np.tile(idx.reshape(-1, 16).T, (8, 1)).astype(np.uint16)


def unstriped(offs):
    return offs[:16].T.reshape(-1).astype(np.int64)


E2M1 = np.array([0.0, 0.5, 1.0, 1.5, 2.0, 3.0, 4.0, 6.0, -0.0, -0.5, -1.0, -1.5, -2.0, -3.0, -4.0, -6.0])


def pack_weight(w, fmt):
    k, n = w.shape
    w = f64(np.asarray(w, np.float32).astype(ml_dtypes.bfloat16)).reshape(k // 32, 32, n)
    amax = np.abs(w).max(1)
    if fmt == "e4m3":
        byte = np.frexp(amax)[1] - 1 + 127 - 7
    elif fmt == "e5m2":
        byte = np.frexp(amax)[1] - 1 + 127 - 14
    else:
        mant, ex = np.frexp(amax / 6.0)
        byte = np.where(mant > 0.5, ex, ex - 1) + 127
    byte = np.clip(np.where(amax > 0, byte, 1), 1, 254)
    scaled = (w * np.exp2(127.0 - byte)[:, None, :]).reshape(k, n).astype(np.float32)
    by_word = np.ascontiguousarray(scaled.reshape(k // 512, 128, 4, n).transpose(0, 1, 3, 2))
    if fmt == "e4m3":
        words = by_word.astype(ml_dtypes.float8_e4m3fn).view(np.uint8)
    elif fmt == "e5m2":
        words = by_word.astype(ml_dtypes.float8_e5m2).view(np.uint8)
    else:
        c = by_word.astype(ml_dtypes.float4_e2m1fn).view(np.uint8) & 0xF
        words = (c[..., 0::2] | (c[..., 1::2] << 4)).reshape(k // 512, 128, 2 * n)
    return np.ascontiguousarray(words), np.ascontiguousarray(byte.astype(np.uint8).reshape(k // 512, 16, n))


def unpack_weight(words, scales, fmt):
    g, _, n = scales.shape
    words = np.ascontiguousarray(words).reshape(g, 128, n, -1)
    if fmt == "e4m3":
        vals = words.view(ml_dtypes.float8_e4m3fn).astype(np.float64)
    elif fmt == "e5m2":
        vals = words.view(ml_dtypes.float8_e5m2).astype(np.float64)
    else:
        nib = np.empty((g, 128, n, 4), np.uint8)
        nib[..., 0::2] = words & 0xF
        nib[..., 1::2] = words >> 4
        vals = E2M1[nib]
    vals = vals * np.repeat(np.exp2(scales.astype(np.float64) - 127.0), 8, axis=1)[..., None]
    return vals.transpose(0, 1, 3, 2).reshape(g * 512, n)


def silu(v):
    return v / (1.0 + np.exp(-np.maximum(v, -700.0)))


def d_silu(v):
    s = 1.0 / (1.0 + np.exp(-np.maximum(v, -700.0)))
    return s * (1.0 + v * (1.0 - s))


K, T, E, C, H, N = 128, 2048, 8, 512, 512, 512


def by_expert(wq, xq):
    return np.concatenate([wq[e].T @ xq[:, e * C:(e + 1) * C] for e in range(E)], axis=1)


def setup_inputs():
    n = np.random.standard_normal
    s = mx_kscale(N)[:, None]
    u = mx_kscale(H)
    first = np.random.permutation(np.repeat(np.arange(E), T // E))
    second = (first + 1 + np.random.permutation(np.repeat(np.arange(E - 1), -(-T // (E - 1)))[:T])) % E
    while np.bincount(second, minlength=E).max() != T // E:
        load = np.bincount(second, minlength=E); hi, lo = int(load.argmax()), int(load.argmin())
        t = np.flatnonzero((second == hi) & (first != lo))[0]; second[t] = lo
    slot_token = np.empty(E * C, np.int64); pos = np.empty((2, T), np.int64); fill = np.zeros(E, np.int64)
    place = np.stack([np.random.permutation(C) for _ in range(E)])
    for r, deal in enumerate((first, second)):
        for t in np.random.permutation(T):
            e = deal[t]; j = e * C + place[e, fill[e]]; fill[e] += 1; slot_token[j] = t; pos[r, t] = j
    g = np.random.uniform(0.2, 0.8, T)
    w_slot = np.empty(E * C); w_slot[pos[0]] = g; w_slot[pos[1]] = 1.0 - g
    dy = pack_weight(n((N, T)) * s, "e5m2")
    return {
        "dy_words": dy[0],
        "dy_scales": dy[1],
        "a1": n((H, E * C)).astype(np.float32),
        "a3": n((H, E * C)).astype(np.float32),
        "w2": (n((E, N, H)) / np.sqrt(N) / s[None] * u[None, None, :]).astype(np.float32),
        "w1": (n((E, H, K)) / np.sqrt(H) / u[None, :, None]).astype(np.float32),
        "w3": (n((E, H, K)) / np.sqrt(H) / u[None, :, None]).astype(np.float32),
        "gate": np.tile(w_slot, (H, 1)).astype(np.float32),
        "offs": striped(slot_token),
        "pos1": striped(pos[0]),
        "pos2": striped(pos[1]),
    }


def reference(dy_words, dy_scales, a1, a3, w2, w1, w3, gate, offs, pos1, pos2):
    idx = unstriped(offs)
    gq = unpack_weight(dy_words, dy_scales, "e5m2")[:, idx]
    dh = f64(gate) * by_expert(mxq(f64(w2), 1, "e4m3"), gq)
    da1 = dh * f64(a3) * d_silu(f64(a1))
    da3 = dh * silu(f64(a1))
    dx = by_expert(mxq(f64(w1), 1, "e4m3"), mxq(da1, 0, "e5m2")) + by_expert(mxq(f64(w3), 1, "e4m3"), mxq(da3, 0, "e5m2"))
    return dx[:, unstriped(pos1)] + dx[:, unstriped(pos2)]

@@ -1,0 +1,257 @@
+from contextlib import ExitStack
+
+import concourse.mybir as mybir
+from concourse.masks import make_identity
+
+K, T, E, C, H, N = 128, 2048, 8, 512, 512, 512
+SLOTS = E * C
+FLOPS = 2 * SLOTS * (N * H + 2 * H * K)
+BYTES = 4 * (2 * H * SLOTS + E * N * H + 2 * E * H * K + SLOTS + K * T) + N * T + 16 * T + 2 * 128 * (256 + 128 + 128)
+
+F32 = mybir.dt.float32
+BF16 = mybir.dt.bfloat16
+I32 = mybir.dt.int32
+U32 = mybir.dt.uint32
+U16 = mybir.dt.uint16
+U8 = mybir.dt.uint8
+E4M3 = mybir.dt.float8_e4m3fn_x4
+E5M2 = mybir.dt.float8_e5m2_x4
+ALU = mybir.AluOpType
+ACT = mybir.ActivationFunctionType
+
+P = 128
+PACK = 4
+BLOCKS = C // P
+LIST_ROWS = 16
+OUT_PIECE = 512
+
+
+def tile_moe_bdx_glu_silu_kernel(
+    tc, dy_words, dy_scales, a1, a3, w2, w1, w3, gate, offs, pos1, pos2, out
+):
+    nc = tc.nc
+    with ExitStack() as ctx:
+        keep = ctx.enter_context(tc.tile_pool(name="keep", bufs=1))
+        ring = ctx.enter_context(tc.tile_pool(name="ring", bufs=2))
+        psum = ctx.enter_context(tc.psum_pool(name="psum", bufs=1))
+
+        offs_sb = keep.tile([P, SLOTS // LIST_ROWS], U16, name="offs_sb")
+        pos1_sb = keep.tile([P, T // LIST_ROWS], U16, name="pos1_sb")
+        pos2_sb = keep.tile([P, T // LIST_ROWS], U16, name="pos2_sb")
+        dyw = keep.tile([P, T], I32, name="dyw", align_bytes=64)
+        dys = keep.tile([P, T], U8, name="dys", align_bytes=64)
+        gate_rows = keep.tile([P, P], F32, name="gate_rows")
+        gate_cols = keep.tile([P, SLOTS // P], F32, name="gate_cols")
+        ident = keep.tile([P, P], F32, name="ident")
+        dx = keep.tile([P, SLOTS], F32, name="dx", align_bytes=64)
+
+        st = [dict() for e in range(E)]
+
+        def load_a1(e):
+            t = ring.tile([P, PACK, C], F32, name="a1_sb", bufs=2)
+            nc.sync.dma_start(out=t[:], in_=a1[:, e * C:(e + 1) * C].rearrange("(p t) c -> p t c", t=PACK))
+            st[e]["a1"] = t
+
+        def load_w2(e):
+            t = ring.tile([P, PACK, H], F32, name="w2_sb", bufs=2)
+            nc.sync.dma_start(out=t[:], in_=w2[e].rearrange("(p j) c -> p j c", j=PACK))
+            st[e]["w2"] = t
+
+        def load_a3(e):
+            t = ring.tile([P, PACK, C], F32, name="a3_sb", bufs=3)
+            nc.sync.dma_start(out=t[:], in_=a3[:, e * C:(e + 1) * C].rearrange("(p t) c -> p t c", t=PACK))
+            st[e]["a3"] = t
+
+        def load_w13(e):
+            t = ring.tile([P, 2, PACK, K], F32, name="w13_sb", bufs=2)
+            nc.sync.dma_start(out=t[:, 0], in_=w1[e].rearrange("(p j) c -> p j c", j=PACK))
+            nc.sync.dma_start(out=t[:, 1], in_=w3[e].rearrange("(p j) c -> p j c", j=PACK))
+            st[e]["w13"] = t
+
+        def gather_words(e):
+            t = ring.tile([P, C], U32, name="g_words", bufs=6, align_bytes=64)
+            cols = slice(e * C // LIST_ROWS, (e + 1) * C // LIST_ROWS)
+            nc.vector.tensor_copy(out=t[:], in_=dyw[:].bitcast(U32).indirect(offs_sb[:, cols]))
+            st[e]["gw"] = t
+
+        def gather_scales(e):
+            t = ring.tile([P, C], U8, name="g_scales", bufs=6, align_bytes=64)
+            cols = slice(e * C // LIST_ROWS, (e + 1) * C // LIST_ROWS)
+            nc.vector.tensor_copy(out=t[:], in_=dys[:].indirect(offs_sb[:, cols]))
+            st[e]["gs"] = t
+
+        def cast_w2(e):
+            t = ring.tile([P, H, PACK], BF16, name="w2_bf", bufs=2, align_bytes=64)
+            nc.scalar.copy(
+                out=t[:].rearrange("p (c i) j -> p c j i", i=2),
+                in_=st[e]["w2"][:].rearrange("p j (c i) -> p c j i", i=2),
+            )
+            st[e]["w2b"] = t
+
+        def cast_w13(e):
+            t = ring.tile([P, 2, K, PACK], BF16, name="w13_bf", bufs=2, align_bytes=64)
+            nc.scalar.copy(
+                out=t[:].rearrange("p m (c i) j -> p m c j i", i=2),
+                in_=st[e]["w13"][:].rearrange("p m j (c i) -> p m c j i", i=2),
+            )
+            st[e]["w13b"] = t
+
+        def quant_w2(e):
+            codes = ring.tile([P, H], U32, name="w2_codes", bufs=2, align_bytes=64)
+            scales = ring.tile([P, H], U8, name="w2_scales", bufs=2, align_bytes=64)
+            nc.vector.quantize_mx(out=codes[:].bitcast(E4M3), scales=scales[:], in_=st[e]["w2b"][:].rearrange("p c j -> p (c j)"))
+            st[e]["w2q"] = (codes, scales)
+
+        def quant_w13(e):
+            codes = ring.tile([P, 2 * K], U32, name="w13_codes", bufs=2, align_bytes=64)
+            scales = ring.tile([P, 2 * K], U8, name="w13_scales", bufs=2, align_bytes=64)
+            nc.vector.quantize_mx(out=codes[:].bitcast(E4M3), scales=scales[:], in_=st[e]["w13b"][:].rearrange("p m c j -> p (m c j)"))
+            st[e]["w13q"] = (codes, scales)
+
+        def activations(e):
+            u = ring.tile([P, PACK, C], F32, name="silu_sb", bufs=3)
+            m = ring.tile([P, PACK, C], F32, name="slope_sb", bufs=3)
+            v = st[e]["a1"]
+            nc.scalar.activation(out=u[:], in_=v[:], func=ACT.Silu)
+            nc.scalar.activation(out=m[:], in_=v[:], func=ACT.Tanh, scale=0.5)
+            nc.scalar.activation(out=m[:], in_=m[:], func=ACT.Copy, scale=-0.5, bias=0.5)
+            st[e]["u"], st[e]["m"] = u, m
+
+        def slope_x(e):
+            u, m = st[e]["u"], st[e]["m"]
+            nc.vector.scalar_tensor_tensor(out=m[:], in0=u[:], scalar=-1.0, in1=m[:], op0=ALU.add, op1=ALU.mult)
+
+        def slope_y(e):
+            m = st[e]["m"]
+            nc.vector.scalar_tensor_tensor(out=m[:], in0=m[:], scalar=1.0, in1=st[e]["a3"][:], op0=ALU.add, op1=ALU.mult)
+
+        def first_product(e):
+            codes, scales = st[e]["w2q"]
+            banks = []
+            for b in range(BLOCKS):
+                cols = slice(b * P, (b + 1) * P)
+                acc = psum.tile([P, H], F32, name="dh_t_ps", bufs=3)
+                nc.tensor.matmul_mx(
+                    out=acc[:], lhsT=st[e]["gw"][:, cols].bitcast(E5M2), lhsT_scale=st[e]["gs"][:, cols],
+                    rhs=codes[:].bitcast(E4M3), rhs_scale=scales[:], start=True, stop=True,
+                )
+                dh_t = ring.tile([P, PACK, P], F32, name="dh_t", bufs=4)
+                g = e * BLOCKS + b
+                nc.scalar.activation(
+                    out=dh_t[:], in_=acc[:].rearrange("p (m t) -> p t m", t=PACK), func=ACT.Copy, scale=gate_cols[:, g:g + 1]
+                )
+                banks.append(dh_t)
+            st[e]["dh_t"] = banks
+
+        def turn(e):
+            banks = []
+            for b in range(BLOCKS):
+                dh = psum.tile([P, PACK, P], F32, name="dh_ps", bufs=4)
+                for t in range(PACK):
+                    nc.tensor.transpose(dh[:, t, :], st[e]["dh_t"][b][:, t, :], ident[:])
+                banks.append(dh)
+            st[e]["dh"] = banks
+
+        def products(e):
+            da3 = ring.tile([P, C, PACK], BF16, name="da3_bf", bufs=2, align_bytes=64)
+            da1 = ring.tile([P, C, PACK], BF16, name="da1_bf", bufs=2, align_bytes=64)
+            for b in range(BLOCKS):
+                cols = slice(b * P, (b + 1) * P)
+                dh = st[e]["dh"][b][:].rearrange("p t (c i) -> p c t i", i=2)
+                for da, f in ((da3, st[e]["u"]), (da1, st[e]["m"])):
+                    nc.vector.tensor_tensor(
+                        out=da[:, cols, :].rearrange("p (c i) t -> p c t i", i=2),
+                        in0=dh,
+                        in1=f[:, :, cols].rearrange("p t (c i) -> p c t i", i=2),
+                        op=ALU.mult,
+                    )
+            st[e]["da"] = (da1, da3)
+
+        def second_product(e):
+            qs = []
+            for m in (1, 0):
+                codes = ring.tile([P, C], U32, name="da_codes", bufs=4, align_bytes=64)
+                scales = ring.tile([P, C], U8, name="da_scales", bufs=4, align_bytes=64)
+                nc.vector.quantize_mx(out=codes[:].bitcast(E5M2), scales=scales[:], in_=st[e]["da"][m][:].rearrange("p c t -> p (c t)"))
+                qs.append((m, codes, scales))
+            wc, ws = st[e]["w13q"]
+            acc = psum.tile([P, C], F32, name="dx_ps", bufs=1)
+            for n, (m, codes, scales) in enumerate(qs):
+                cols = slice(m * K, (m + 1) * K)
+                nc.tensor.matmul_mx(
+                    out=acc[:], lhsT=wc[:, cols].bitcast(E4M3), lhsT_scale=ws[:, cols],
+                    rhs=codes[:].bitcast(E5M2), rhs_scale=scales[:], start=(n == 0), stop=(n == 1),
+                )
+            st[e]["dx"] = acc
+
+        def keep_dx(e):
+            nc.scalar.copy(out=dx[:, e * C:(e + 1) * C], in_=st[e]["dx"][:])
+
+        nc.vector.memset(dys[:].bitcast(I32), 0)
+        nc.gpsimd.memset(gate_rows[32:64, :], 0.0)
+        nc.gpsimd.memset(gate_rows[64:128, :], 0.0)
+        make_identity(nc, ident[:])
+
+        load_a1(0)
+        nc.sync.dma_start(offs_sb[:], offs)
+        nc.sync.dma_start(out=dyw[:], in_=dy_words[0].rearrange("p n t -> p (n t)").bitcast(I32))
+        for q in range(4):
+            nc.sync.dma_start(out=dys[32 * q:32 * q + 4, :].bitcast(I32), in_=dy_scales[0, 4 * q:4 * q + 4, :].bitcast(I32))
+        load_w2(0)
+        nc.sync.dma_start(out=gate_rows[0:32, :], in_=gate[0].rearrange("(b p) -> b p", p=P))
+        load_a3(0)
+        load_w13(0)
+
+        gate_ps = psum.tile([P, PACK, P], F32, name="dh_ps", bufs=4)
+        nc.tensor.transpose(gate_ps[:, 0, :], gate_rows[:], ident[:])
+        nc.scalar.copy(out=gate_cols[:], in_=gate_ps[:, 0, 0:SLOTS // P])
+
+        gather_words(0)
+        gather_scales(0)
+        activations(0)
+        cast_w2(0)
+        quant_w2(0)
+        for e in range(E):
+            more = e + 1 < E
+            if more:
+                load_a1(e + 1)
+                load_w2(e + 1)
+                load_a3(e + 1)
+                load_w13(e + 1)
+            if e == 1:
+                nc.sync.dma_start(pos1_sb[:], pos1)
+                nc.sync.dma_start(pos2_sb[:], pos2)
+            first_product(e)
+            if e > 0:
+                keep_dx(e - 1)
+            turn(e)
+            cast_w13(e)
+            slope_x(e)
+            if more:
+                gather_words(e + 1)
+            slope_y(e)
+            if more:
+                cast_w2(e + 1)
+                activations(e + 1)
+                gather_scales(e + 1)
+            products(e)
+            quant_w13(e)
+            if more:
+                quant_w2(e + 1)
+            second_product(e)
+        keep_dx(E - 1)
+
+        pieces = T // OUT_PIECE
+        firsts = []
+        for i in range(pieces + 1):
+            if i < pieces:
+                cols = slice(i * OUT_PIECE // LIST_ROWS, (i + 1) * OUT_PIECE // LIST_ROWS)
+                first = ring.tile([P, OUT_PIECE], F32, name="first", bufs=2)
+                nc.vector.tensor_copy(out=first[:], in_=dx[:].indirect(pos1_sb[:, cols]))
+                firsts.append(first)
+            if i > 0:
+                j = i - 1
+                cols = slice(j * OUT_PIECE // LIST_ROWS, (j + 1) * OUT_PIECE // LIST_ROWS)
+                both = ring.tile([P, OUT_PIECE], F32, name="both", bufs=4)
+                nc.vector.tensor_tensor(out=both[:], in0=dx[:].indirect(pos2_sb[:, cols]), in1=firsts[j][:], op=ALU.add)
+                nc.sync.dma_start(out=out[:, j * OUT_PIECE:(j + 1) * OUT_PIECE], in_=both[:])

@@ -24,6 +24,10 @@ PACK = 4
 BLOCKS = C // P
 LIST_ROWS = 16
 OUT_PIECE = 512
+GX = 0
+AS = 2048
+GP = 512
+W = PACK * C
 
 
 def tile_moe_bdx_glu_silu_kernel(
@@ -49,7 +53,10 @@ def tile_moe_bdx_glu_silu_kernel(
 
         def load_a1(e):
             t = ring.tile([P, PACK, C], F32, name="a1_sb", bufs=2)
-            nc.sync.dma_start(out=t[:], in_=a1[:, e * C:(e + 1) * C].rearrange("(p t) c -> p t c", t=PACK))
+            src = a1[:, e * C:(e + 1) * C].rearrange("(p t) c -> p t c", t=PACK)
+            step = PACK // (1 if e == 0 else 1)
+            for t0 in range(0, PACK, step):
+                nc.sync.dma_start(out=t[:, t0:t0 + step, :], in_=src[:, t0:t0 + step, :])
             st[e]["a1"] = t
 
         def load_w2(e):
@@ -58,7 +65,7 @@ def tile_moe_bdx_glu_silu_kernel(
             st[e]["w2"] = t
 
         def load_a3(e):
-            t = ring.tile([P, PACK, C], F32, name="a3_sb", bufs=3)
+            t = ring.tile([P, PACK, C], F32, name="a3_sb", bufs=2)
             nc.sync.dma_start(out=t[:], in_=a3[:, e * C:(e + 1) * C].rearrange("(p t) c -> p t c", t=PACK))
             st[e]["a3"] = t
 
@@ -69,13 +76,13 @@ def tile_moe_bdx_glu_silu_kernel(
             st[e]["w13"] = t
 
         def gather_words(e):
-            t = ring.tile([P, C], U32, name="g_words", bufs=6, align_bytes=64)
+            t = ring.tile([P, C], U32, name="g_words", bufs=4, align_bytes=64)
             cols = slice(e * C // LIST_ROWS, (e + 1) * C // LIST_ROWS)
             nc.vector.tensor_copy(out=t[:], in_=dyw[:].bitcast(U32).indirect(offs_sb[:, cols]))
             st[e]["gw"] = t
 
         def gather_scales(e):
-            t = ring.tile([P, C], U8, name="g_scales", bufs=6, align_bytes=64)
+            t = ring.tile([P, C], U8, name="g_scales", bufs=4, align_bytes=64)
             cols = slice(e * C // LIST_ROWS, (e + 1) * C // LIST_ROWS)
             nc.vector.tensor_copy(out=t[:], in_=dys[:].indirect(offs_sb[:, cols]))
             st[e]["gs"] = t
@@ -109,13 +116,16 @@ def tile_moe_bdx_glu_silu_kernel(
             st[e]["w13q"] = (codes, scales)
 
         def activations(e):
-            u = ring.tile([P, PACK, C], F32, name="silu_sb", bufs=3)
-            m = ring.tile([P, PACK, C], F32, name="slope_sb", bufs=3)
-            v = st[e]["a1"]
-            nc.scalar.activation(out=u[:], in_=v[:], func=ACT.Silu)
-            nc.scalar.activation(out=m[:], in_=v[:], func=ACT.Tanh, scale=0.5)
-            nc.scalar.activation(out=m[:], in_=m[:], func=ACT.Copy, scale=-0.5, bias=0.5)
+            u = ring.tile([P, W], F32, name="silu_sb", bufs=3)
+            m = ring.tile([P, W], F32, name="slope_sb", bufs=3)
+            v = st[e]["a1"][:].rearrange("p t c -> p (t c)")
+            calls = [(u, ACT.Silu, 1.0), (m, ACT.Sigmoid, -1.0)]
+            for dst, func, scale in (calls if e % 2 == 0 else calls[::-1]):
+                nc.scalar.activation(out=dst[:], in_=v, func=func, scale=scale)
             st[e]["u"], st[e]["m"] = u, m
+
+        def slope_m(e):
+            return
 
         def slope_x(e):
             u, m = st[e]["u"], st[e]["m"]
@@ -123,19 +133,21 @@ def tile_moe_bdx_glu_silu_kernel(
 
         def slope_y(e):
             m = st[e]["m"]
-            nc.vector.scalar_tensor_tensor(out=m[:], in0=m[:], scalar=1.0, in1=st[e]["a3"][:], op0=ALU.add, op1=ALU.mult)
+            b = st[e]["a3"][:].rearrange("p t c -> p (t c)")
+            nc.vector.scalar_tensor_tensor(out=m[:], in0=m[:], scalar=1.0, in1=b, op0=ALU.add, op1=ALU.mult)
+            st[e]["y"] = m
 
         def first_product(e):
             codes, scales = st[e]["w2q"]
             banks = []
             for b in range(BLOCKS):
                 cols = slice(b * P, (b + 1) * P)
-                acc = psum.tile([P, H], F32, name="dh_t_ps", bufs=3)
+                acc = psum.tile([P, H], F32, name="dh_t_ps", bufs=4 - 1)
                 nc.tensor.matmul_mx(
                     out=acc[:], lhsT=st[e]["gw"][:, cols].bitcast(E5M2), lhsT_scale=st[e]["gs"][:, cols],
                     rhs=codes[:].bitcast(E4M3), rhs_scale=scales[:], start=True, stop=True,
                 )
-                dh_t = ring.tile([P, PACK, P], F32, name="dh_t", bufs=4)
+                dh_t = ring.tile([P, PACK, P], F32, name="dh_t", bufs=8)
                 g = e * BLOCKS + b
                 nc.scalar.activation(
                     out=dh_t[:], in_=acc[:].rearrange("p (m t) -> p t m", t=PACK), func=ACT.Copy, scale=gate_cols[:, g:g + 1]
@@ -158,11 +170,11 @@ def tile_moe_bdx_glu_silu_kernel(
             for b in range(BLOCKS):
                 cols = slice(b * P, (b + 1) * P)
                 dh = st[e]["dh"][b][:].rearrange("p t (c i) -> p c t i", i=2)
-                for da, f in ((da3, st[e]["u"]), (da1, st[e]["m"])):
+                for da, f in ((da3, st[e]["u"]), (da1, st[e]["y"])):
                     nc.vector.tensor_tensor(
                         out=da[:, cols, :].rearrange("p (c i) t -> p c t i", i=2),
                         in0=dh,
-                        in1=f[:, :, cols].rearrange("p t (c i) -> p c t i", i=2),
+                        in1=f[:].rearrange("p (t c) -> p t c", t=PACK)[:, :, cols].rearrange("p t (c i) -> p c t i", i=2),
                         op=ALU.mult,
                     )
             st[e]["da"] = (da1, da3)
@@ -192,13 +204,26 @@ def tile_moe_bdx_glu_silu_kernel(
         nc.gpsimd.memset(gate_rows[64:128, :], 0.0)
         make_identity(nc, ident[:])
 
+        def load_offs():
+            nc.sync.dma_start(offs_sb[:], offs)
+
+        def load_dy():
+            nc.sync.dma_start(out=dyw[:], in_=dy_words[0].rearrange("p n t -> p (n t)").bitcast(I32))
+
+        def load_sc():
+            for q in range(4):
+                nc.sync.dma_start(out=dys[32 * q:32 * q + 4, :].bitcast(I32), in_=dy_scales[0, 4 * q:4 * q + 4, :].bitcast(I32))
+
+        def load_gate():
+            nc.sync.dma_start(out=gate_rows[0:32, :], in_=gate[0].rearrange("(b p) -> b p", p=P))
+
+        load_offs()
+        load_gate()
+        load_sc()
         load_a1(0)
-        nc.sync.dma_start(offs_sb[:], offs)
-        nc.sync.dma_start(out=dyw[:], in_=dy_words[0].rearrange("p n t -> p (n t)").bitcast(I32))
-        for q in range(4):
-            nc.sync.dma_start(out=dys[32 * q:32 * q + 4, :].bitcast(I32), in_=dy_scales[0, 4 * q:4 * q + 4, :].bitcast(I32))
+        load_dy()
         load_w2(0)
-        nc.sync.dma_start(out=gate_rows[0:32, :], in_=gate[0].rearrange("(b p) -> b p", p=P))
+        load_a1(1)
         load_a3(0)
         load_w13(0)
 
@@ -206,52 +231,75 @@ def tile_moe_bdx_glu_silu_kernel(
         nc.tensor.transpose(gate_ps[:, 0, :], gate_rows[:], ident[:])
         nc.scalar.copy(out=gate_cols[:], in_=gate_ps[:, 0, 0:SLOTS // P])
 
+        def loads(e):
+            if 2 == 1:
+                load_a1(e)
+            load_w2(e)
+            if 2 == 2 and e + 1 < E:
+                load_a1(e + 1)
+            load_a3(e)
+            load_w13(e)
+
         gather_words(0)
         gather_scales(0)
         activations(0)
         cast_w2(0)
         quant_w2(0)
+        first_product(0)
+        loads(1)
+        gather_words(1)
+        gather_scales(1)
+        if 2 == 2:
+            activations(1)
+        cast_w2(1)
+        cast_w13(0)
+        quant_w2(1)
+        quant_w13(0)
+        nc.sync.dma_start(pos1_sb[:], pos1)
+        nc.sync.dma_start(pos2_sb[:], pos2)
         for e in range(E):
-            more = e + 1 < E
-            if more:
-                load_a1(e + 1)
-                load_w2(e + 1)
-                load_a3(e + 1)
-                load_w13(e + 1)
-            if e == 1:
-                nc.sync.dma_start(pos1_sb[:], pos1)
-                nc.sync.dma_start(pos2_sb[:], pos2)
-            first_product(e)
+            if e + 2 < E:
+                loads(e + 2)
+            slope_m(e)
+            slope_x(e)
+            slope_y(e)
+            turn(e)
+            if e + 1 < E:
+                if 2 == 1:
+                    activations(e + 1)
+                first_product(e + 1)
+            if e + 2 < E:
+                cast_w2(e + 2)
+            if e + 1 < E:
+                cast_w13(e + 1)
+            if 2 == 2 and e + 2 < E:
+                activations(e + 2)
             if e > 0:
                 keep_dx(e - 1)
-            turn(e)
-            cast_w13(e)
-            slope_x(e)
-            if more:
-                gather_words(e + 1)
-            slope_y(e)
-            if more:
-                cast_w2(e + 1)
-                activations(e + 1)
-                gather_scales(e + 1)
             products(e)
-            quant_w13(e)
-            if more:
-                quant_w2(e + 1)
+            if e + 2 < E:
+                gather_words(e + 2)
+                gather_scales(e + 2)
             second_product(e)
+            if e + 2 < E:
+                quant_w2(e + 2)
+            if e + 1 < E:
+                quant_w13(e + 1)
         keep_dx(E - 1)
 
-        pieces = T // OUT_PIECE
         firsts = []
-        for i in range(pieces + 1):
-            if i < pieces:
-                cols = slice(i * OUT_PIECE // LIST_ROWS, (i + 1) * OUT_PIECE // LIST_ROWS)
-                first = ring.tile([P, OUT_PIECE], F32, name="first", bufs=2)
-                nc.vector.tensor_copy(out=first[:], in_=dx[:].indirect(pos1_sb[:, cols]))
-                firsts.append(first)
-            if i > 0:
-                j = i - 1
-                cols = slice(j * OUT_PIECE // LIST_ROWS, (j + 1) * OUT_PIECE // LIST_ROWS)
-                both = ring.tile([P, OUT_PIECE], F32, name="both", bufs=4)
-                nc.vector.tensor_tensor(out=both[:], in0=dx[:].indirect(pos2_sb[:, cols]), in1=firsts[j][:], op=ALU.add)
-                nc.sync.dma_start(out=out[:, j * OUT_PIECE:(j + 1) * OUT_PIECE], in_=both[:])
+        for c0 in range(0, T, OUT_PIECE):
+            first = ring.tile([P, OUT_PIECE], F32, name="first", tag="dh_t", bufs=8)
+            cols = slice(c0 // LIST_ROWS, (c0 + OUT_PIECE) // LIST_ROWS)
+            nc.vector.tensor_copy(out=first[:], in_=dx[:].indirect(pos1_sb[:, cols]))
+            firsts.append(first)
+        c0 = 0
+        for width in (512, 512, 512, 384, 128):
+            both = ring.tile([P, width], F32, name="both", tag="dh_t", bufs=8)
+            cols = slice(c0 // LIST_ROWS, (c0 + width) // LIST_ROWS)
+            local = c0 % OUT_PIECE
+            nc.vector.tensor_tensor(
+                out=both[:], in0=dx[:].indirect(pos2_sb[:, cols]), in1=firsts[c0 // OUT_PIECE][:, local:local + width], op=ALU.add
+            )
+            nc.sync.dma_start(out=out[:, c0:c0 + width], in_=both[:])
+            c0 = c0 + width

@@ -25,8 +25,8 @@ BLOCKS = C // P
 LIST_ROWS = 16
 OUT_PIECE = 512
 GX = 0
-AS = 2048
-GP = 512
+AS = 0
+GP = 1024
 W = PACK * C
 
 
@@ -117,25 +117,47 @@ def tile_moe_bdx_glu_silu_kernel(
 
         def activations(e):
             u = ring.tile([P, W], F32, name="silu_sb", bufs=3)
-            m = ring.tile([P, W], F32, name="slope_sb", bufs=3)
+            th = ring.tile([P, W], F32, name="tanh_sb", bufs=2)
             v = st[e]["a1"][:].rearrange("p t c -> p (t c)")
-            calls = [(u, ACT.Silu, 1.0), (m, ACT.Sigmoid, -1.0)]
-            for dst, func, scale in (calls if e % 2 == 0 else calls[::-1]):
-                nc.scalar.activation(out=dst[:], in_=v, func=func, scale=scale)
-            st[e]["u"], st[e]["m"] = u, m
+            step = W // (1 if e == 0 else 1)
+            for c0 in range(0, W, step):
+                nc.scalar.activation(out=u[:, c0:c0 + step], in_=v[:, c0:c0 + step], func=ACT.Silu)
+                nc.scalar.activation(out=th[:, c0:c0 + step], in_=v[:, c0:c0 + step], func=ACT.Tanh, scale=0.5)
+            gx = GX if e >= 1 else 0
+            if gx:
+                less = ring.tile([P, gx], F32, name="silu_less_one", bufs=2)
+                nc.scalar.activation(out=less[:], in_=u[:, 0:gx], func=ACT.Copy, bias=-1.0)
+                st[e]["less"] = less
+            sa = min(AS, gx)
+            if sa:
+                nc.scalar.activation(out=th[:, 0:sa], in_=th[:, 0:sa], func=ACT.Copy, scale=-0.5, bias=0.5)
+            st[e]["u"], st[e]["th"], st[e]["gx"], st[e]["sa"] = u, th, gx, sa
 
         def slope_m(e):
-            return
+            th, gx, sa = st[e]["th"], st[e]["gx"], st[e]["sa"]
+            m = ring.tile([P, W], F32, name="slope_sb", bufs=1)
+            for c0 in range(0, sa, 256):
+                cols = slice(c0, min(c0 + 256, sa))
+                nc.gpsimd.tensor_tensor(out=m[:, cols], in0=st[e]["less"][:, cols], in1=th[:, cols], op=ALU.mult)
+            for c0 in range(sa, W, GP):
+                cols = slice(c0, min(c0 + GP, W))
+                nc.gpsimd.tensor_scalar(out=m[:, cols], in0=th[:, cols], scalar1=-0.5, scalar2=0.5, op0=ALU.mult, op1=ALU.add)
+            for c0 in range(sa, gx, 256):
+                cols = slice(c0, min(c0 + 256, gx))
+                nc.gpsimd.tensor_tensor(out=m[:, cols], in0=st[e]["less"][:, cols], in1=m[:, cols], op=ALU.mult)
+            st[e]["m"] = m
 
         def slope_x(e):
-            u, m = st[e]["u"], st[e]["m"]
-            nc.vector.scalar_tensor_tensor(out=m[:], in0=u[:], scalar=-1.0, in1=m[:], op0=ALU.add, op1=ALU.mult)
+            gx = st[e]["gx"]
+            uf = st[e]["u"][:, gx:W]
+            mf = st[e]["m"][:, gx:W]
+            nc.vector.scalar_tensor_tensor(out=mf, in0=uf, scalar=-1.0, in1=mf, op0=ALU.add, op1=ALU.mult)
 
         def slope_y(e):
-            m = st[e]["m"]
+            y = ring.tile([P, W], F32, name="factor_sb", bufs=2)
             b = st[e]["a3"][:].rearrange("p t c -> p (t c)")
-            nc.vector.scalar_tensor_tensor(out=m[:], in0=m[:], scalar=1.0, in1=b, op0=ALU.add, op1=ALU.mult)
-            st[e]["y"] = m
+            nc.vector.scalar_tensor_tensor(out=y[:], in0=st[e]["m"][:], scalar=1.0, in1=b, op0=ALU.add, op1=ALU.mult)
+            st[e]["y"] = y
 
         def first_product(e):
             codes, scales = st[e]["w2q"]

@@ -24,7 +24,7 @@ PACK = 4
 BLOCKS = C // P
 LIST_ROWS = 16
 OUT_PIECE = 512
-GX = 0
+GX = 512
 AS = 0
 GP = 1024
 W = PACK * C
@@ -75,17 +75,18 @@ def tile_moe_bdx_glu_silu_kernel(
             nc.sync.dma_start(out=t[:, 1], in_=w3[e].rearrange("(p j) c -> p j c", j=PACK))
             st[e]["w13"] = t
 
-        def gather_words(e):
-            t = ring.tile([P, C], U32, name="g_words", bufs=4, align_bytes=64)
-            cols = slice(e * C // LIST_ROWS, (e + 1) * C // LIST_ROWS)
-            nc.vector.tensor_copy(out=t[:], in_=dyw[:].bitcast(U32).indirect(offs_sb[:, cols]))
-            st[e]["gw"] = t
-
-        def gather_scales(e):
-            t = ring.tile([P, C], U8, name="g_scales", bufs=4, align_bytes=64)
-            cols = slice(e * C // LIST_ROWS, (e + 1) * C // LIST_ROWS)
-            nc.vector.tensor_copy(out=t[:], in_=dys[:].indirect(offs_sb[:, cols]))
-            st[e]["gs"] = t
+        def gathers(e):
+            if e % 2:
+                return
+            n = 2 * C
+            cols = slice(e * C // LIST_ROWS, (e * C + n) // LIST_ROWS)
+            words = ring.tile([P, n], U32, name="g_words", bufs=4 // 2, align_bytes=64)
+            nc.vector.tensor_copy(out=words[:], in_=dyw[:].bitcast(U32).indirect(offs_sb[:, cols]))
+            scales = ring.tile([P, n], U8, name="g_scales", bufs=4 // 2, align_bytes=64)
+            nc.vector.tensor_copy(out=scales[:], in_=dys[:].indirect(offs_sb[:, cols]))
+            for f in range(2):
+                st[e + f]["gw"] = words[:, f * C:(f + 1) * C]
+                st[e + f]["gs"] = scales[:, f * C:(f + 1) * C]
 
         def cast_w2(e):
             t = ring.tile([P, H, PACK], BF16, name="w2_bf", bufs=2, align_bytes=64)
@@ -121,9 +122,12 @@ def tile_moe_bdx_glu_silu_kernel(
             v = st[e]["a1"][:].rearrange("p t c -> p (t c)")
             step = W // (1 if e == 0 else 1)
             for c0 in range(0, W, step):
-                nc.scalar.activation(out=u[:, c0:c0 + step], in_=v[:, c0:c0 + step], func=ACT.Silu)
+                if e == 0 or not 0:
+                    nc.scalar.activation(out=u[:, c0:c0 + step], in_=v[:, c0:c0 + step], func=ACT.Silu)
                 nc.scalar.activation(out=th[:, c0:c0 + step], in_=v[:, c0:c0 + step], func=ACT.Tanh, scale=0.5)
-            gx = GX if e >= 1 else 0
+                if e > 0 and 0:
+                    nc.scalar.activation(out=u[:, c0:c0 + step], in_=v[:, c0:c0 + step], func=ACT.Silu)
+            gx = GX if e >= 3 else 0
             if gx:
                 less = ring.tile([P, gx], F32, name="silu_less_one", bufs=2)
                 nc.scalar.activation(out=less[:], in_=u[:, 0:gx], func=ACT.Copy, bias=-1.0)
@@ -136,27 +140,32 @@ def tile_moe_bdx_glu_silu_kernel(
         def slope_m(e):
             th, gx, sa = st[e]["th"], st[e]["gx"], st[e]["sa"]
             m = ring.tile([P, W], F32, name="slope_sb", bufs=1)
-            for c0 in range(0, sa, 256):
-                cols = slice(c0, min(c0 + 256, sa))
+            for c0 in range(0, sa, 512):
+                cols = slice(c0, min(c0 + 512, sa))
                 nc.gpsimd.tensor_tensor(out=m[:, cols], in0=st[e]["less"][:, cols], in1=th[:, cols], op=ALU.mult)
             for c0 in range(sa, W, GP):
                 cols = slice(c0, min(c0 + GP, W))
                 nc.gpsimd.tensor_scalar(out=m[:, cols], in0=th[:, cols], scalar1=-0.5, scalar2=0.5, op0=ALU.mult, op1=ALU.add)
-            for c0 in range(sa, gx, 256):
-                cols = slice(c0, min(c0 + 256, gx))
+            for c0 in range(sa, gx, 512):
+                cols = slice(c0, min(c0 + 512, gx))
                 nc.gpsimd.tensor_tensor(out=m[:, cols], in0=st[e]["less"][:, cols], in1=m[:, cols], op=ALU.mult)
             st[e]["m"] = m
 
         def slope_x(e):
             gx = st[e]["gx"]
-            uf = st[e]["u"][:, gx:W]
-            mf = st[e]["m"][:, gx:W]
-            nc.vector.scalar_tensor_tensor(out=mf, in0=uf, scalar=-1.0, in1=mf, op0=ALU.add, op1=ALU.mult)
+            step = (W - gx) // 1
+            for c0 in range(gx, W, step):
+                uf = st[e]["u"][:, c0:c0 + step]
+                mf = st[e]["m"][:, c0:c0 + step]
+                nc.vector.scalar_tensor_tensor(out=mf, in0=uf, scalar=-1.0, in1=mf, op0=ALU.add, op1=ALU.mult)
 
         def slope_y(e):
             y = ring.tile([P, W], F32, name="factor_sb", bufs=2)
             b = st[e]["a3"][:].rearrange("p t c -> p (t c)")
-            nc.vector.scalar_tensor_tensor(out=y[:], in0=st[e]["m"][:], scalar=1.0, in1=b, op0=ALU.add, op1=ALU.mult)
+            step = W // 1
+            for c0 in range(0, W, step):
+                cols = slice(c0, c0 + step)
+                nc.vector.scalar_tensor_tensor(out=y[:, cols], in0=st[e]["m"][:, cols], scalar=1.0, in1=b[:, cols], op0=ALU.add, op1=ALU.mult)
             st[e]["y"] = y
 
         def first_product(e):
@@ -221,7 +230,7 @@ def tile_moe_bdx_glu_silu_kernel(
         def keep_dx(e):
             nc.scalar.copy(out=dx[:, e * C:(e + 1) * C], in_=st[e]["dx"][:])
 
-        nc.vector.memset(dys[:].bitcast(I32), 0)
+        nc.gpsimd.memset(dys[:].bitcast(I32), 0)
         nc.gpsimd.memset(gate_rows[32:64, :], 0.0)
         nc.gpsimd.memset(gate_rows[64:128, :], 0.0)
         make_identity(nc, ident[:])
@@ -254,29 +263,27 @@ def tile_moe_bdx_glu_silu_kernel(
         nc.scalar.copy(out=gate_cols[:], in_=gate_ps[:, 0, 0:SLOTS // P])
 
         def loads(e):
-            if 2 == 1:
+            if "a1" not in st[e]:
                 load_a1(e)
             load_w2(e)
-            if 2 == 2 and e + 1 < E:
+            if 1 and e + 1 < E:
                 load_a1(e + 1)
             load_a3(e)
             load_w13(e)
 
-        gather_words(0)
-        gather_scales(0)
+        gathers(0)
         activations(0)
         cast_w2(0)
         quant_w2(0)
         first_product(0)
         loads(1)
-        gather_words(1)
-        gather_scales(1)
-        if 2 == 2:
-            activations(1)
+        gathers(1)
+        activations(1)
         cast_w2(1)
         cast_w13(0)
-        quant_w2(1)
-        quant_w13(0)
+        if not 0:
+            quant_w2(1)
+            quant_w13(0)
         nc.sync.dma_start(pos1_sb[:], pos1)
         nc.sync.dma_start(pos2_sb[:], pos2)
         for e in range(E):
@@ -286,27 +293,32 @@ def tile_moe_bdx_glu_silu_kernel(
             slope_x(e)
             slope_y(e)
             turn(e)
-            if e + 1 < E:
-                if 2 == 1:
-                    activations(e + 1)
+            if e + 1 < E and not 0:
                 first_product(e + 1)
+            if 0 and e + 2 < E:
+                activations(e + 2)
             if e + 2 < E:
                 cast_w2(e + 2)
             if e + 1 < E:
                 cast_w13(e + 1)
-            if 2 == 2 and e + 2 < E:
+            if not 0 and e + 2 < E:
                 activations(e + 2)
             if e > 0:
                 keep_dx(e - 1)
             products(e)
+            if 0:
+                if e + 1 < E:
+                    quant_w2(e + 1)
+                    first_product(e + 1)
+                quant_w13(e)
             if e + 2 < E:
-                gather_words(e + 2)
-                gather_scales(e + 2)
+                gathers(e + 2)
             second_product(e)
-            if e + 2 < E:
-                quant_w2(e + 2)
-            if e + 1 < E:
-                quant_w13(e + 1)
+            if not 0:
+                if e + 2 < E:
+                    quant_w2(e + 2)
+                if e + 1 < E:
+                    quant_w13(e + 1)
         keep_dx(E - 1)
 
         firsts = []

from contextlib import ExitStack

import concourse.mybir as mybir
from concourse.masks import make_identity

K, T, E, C, H, N = 128, 2048, 8, 512, 512, 512
SLOTS = E * C
FLOPS = 2 * SLOTS * (N * H + 2 * H * K)
BYTES = 4 * (2 * H * SLOTS + E * N * H + 2 * E * H * K + SLOTS + K * T) + N * T + 16 * T + 2 * 128 * (256 + 128 + 128)

F32 = mybir.dt.float32
BF16 = mybir.dt.bfloat16
I32 = mybir.dt.int32
U32 = mybir.dt.uint32
U16 = mybir.dt.uint16
U8 = mybir.dt.uint8
E4M3 = mybir.dt.float8_e4m3fn_x4
E5M2 = mybir.dt.float8_e5m2_x4
ALU = mybir.AluOpType
ACT = mybir.ActivationFunctionType

P = 128
PACK = 4
BLOCKS = C // P
LIST_ROWS = 16
OUT_PIECE = 512
GX = 512
AS = 0
GP = 1024
W = PACK * C


def tile_moe_bdx_glu_silu_kernel(
    tc, dy_words, dy_scales, a1, a3, w2, w1, w3, gate, offs, pos1, pos2, out
):
    nc = tc.nc
    with ExitStack() as ctx:
        keep = ctx.enter_context(tc.tile_pool(name="keep", bufs=1))
        ring = ctx.enter_context(tc.tile_pool(name="ring", bufs=2))
        psum = ctx.enter_context(tc.psum_pool(name="psum", bufs=1))

        offs_sb = keep.tile([P, SLOTS // LIST_ROWS], U16, name="offs_sb")
        pos1_sb = keep.tile([P, T // LIST_ROWS], U16, name="pos1_sb")
        pos2_sb = keep.tile([P, T // LIST_ROWS], U16, name="pos2_sb")
        dyw = keep.tile([P, T], I32, name="dyw", align_bytes=64)
        dys = keep.tile([P, T], U8, name="dys", align_bytes=64)
        gate_rows = keep.tile([P, P], F32, name="gate_rows")
        gate_cols = keep.tile([P, SLOTS // P], F32, name="gate_cols")
        ident = keep.tile([P, P], F32, name="ident")
        dx = keep.tile([P, SLOTS], F32, name="dx", align_bytes=64)

        st = [dict() for e in range(E)]

        def load_a1(e):
            t = ring.tile([P, PACK, C], F32, name="a1_sb", bufs=2)
            src = a1[:, e * C:(e + 1) * C].rearrange("(p t) c -> p t c", t=PACK)
            step = PACK // (1 if e == 0 else 1)
            for t0 in range(0, PACK, step):
                nc.sync.dma_start(out=t[:, t0:t0 + step, :], in_=src[:, t0:t0 + step, :])
            st[e]["a1"] = t

        def load_w2(e):
            t = ring.tile([P, PACK, H], F32, name="w2_sb", bufs=2)
            nc.sync.dma_start(out=t[:], in_=w2[e].rearrange("(p j) c -> p j c", j=PACK))
            st[e]["w2"] = t

        def load_a3(e):
            t = ring.tile([P, PACK, C], F32, name="a3_sb", bufs=2)
            nc.sync.dma_start(out=t[:], in_=a3[:, e * C:(e + 1) * C].rearrange("(p t) c -> p t c", t=PACK))
            st[e]["a3"] = t

        def load_w13(e):
            t = ring.tile([P, 2, PACK, K], F32, name="w13_sb", bufs=2)
            nc.sync.dma_start(out=t[:, 0], in_=w1[e].rearrange("(p j) c -> p j c", j=PACK))
            nc.sync.dma_start(out=t[:, 1], in_=w3[e].rearrange("(p j) c -> p j c", j=PACK))
            st[e]["w13"] = t

        def gathers(e):
            if e % 2:
                return
            n = 2 * C
            cols = slice(e * C // LIST_ROWS, (e * C + n) // LIST_ROWS)
            words = ring.tile([P, n], U32, name="g_words", bufs=4 // 2, align_bytes=64)
            nc.vector.tensor_copy(out=words[:], in_=dyw[:].bitcast(U32).indirect(offs_sb[:, cols]))
            scales = ring.tile([P, n], U8, name="g_scales", bufs=4 // 2, align_bytes=64)
            nc.vector.tensor_copy(out=scales[:], in_=dys[:].indirect(offs_sb[:, cols]))
            for f in range(2):
                st[e + f]["gw"] = words[:, f * C:(f + 1) * C]
                st[e + f]["gs"] = scales[:, f * C:(f + 1) * C]

        def cast_w2(e):
            t = ring.tile([P, H, PACK], BF16, name="w2_bf", bufs=2, align_bytes=64)
            nc.scalar.copy(
                out=t[:].rearrange("p (c i) j -> p c j i", i=2),
                in_=st[e]["w2"][:].rearrange("p j (c i) -> p c j i", i=2),
            )
            st[e]["w2b"] = t

        def cast_w13(e):
            t = ring.tile([P, 2, K, PACK], BF16, name="w13_bf", bufs=2, align_bytes=64)
            nc.scalar.copy(
                out=t[:].rearrange("p m (c i) j -> p m c j i", i=2),
                in_=st[e]["w13"][:].rearrange("p m j (c i) -> p m c j i", i=2),
            )
            st[e]["w13b"] = t

        def quant_w2(e):
            codes = ring.tile([P, H], U32, name="w2_codes", bufs=2, align_bytes=64)
            scales = ring.tile([P, H], U8, name="w2_scales", bufs=2, align_bytes=64)
            nc.vector.quantize_mx(out=codes[:].bitcast(E4M3), scales=scales[:], in_=st[e]["w2b"][:].rearrange("p c j -> p (c j)"))
            st[e]["w2q"] = (codes, scales)

        def quant_w13(e):
            codes = ring.tile([P, 2 * K], U32, name="w13_codes", bufs=2, align_bytes=64)
            scales = ring.tile([P, 2 * K], U8, name="w13_scales", bufs=2, align_bytes=64)
            nc.vector.quantize_mx(out=codes[:].bitcast(E4M3), scales=scales[:], in_=st[e]["w13b"][:].rearrange("p m c j -> p (m c j)"))
            st[e]["w13q"] = (codes, scales)

        def activations(e):
            u = ring.tile([P, W], F32, name="silu_sb", bufs=3)
            th = ring.tile([P, W], F32, name="tanh_sb", bufs=2)
            v = st[e]["a1"][:].rearrange("p t c -> p (t c)")
            step = W // (1 if e == 0 else 1)
            for c0 in range(0, W, step):
                if e == 0 or not 0:
                    nc.scalar.activation(out=u[:, c0:c0 + step], in_=v[:, c0:c0 + step], func=ACT.Silu)
                nc.scalar.activation(out=th[:, c0:c0 + step], in_=v[:, c0:c0 + step], func=ACT.Tanh, scale=0.5)
                if e > 0 and 0:
                    nc.scalar.activation(out=u[:, c0:c0 + step], in_=v[:, c0:c0 + step], func=ACT.Silu)
            gx = GX if e >= 3 else 0
            if gx:
                less = ring.tile([P, gx], F32, name="silu_less_one", bufs=2)
                nc.scalar.activation(out=less[:], in_=u[:, 0:gx], func=ACT.Copy, bias=-1.0)
                st[e]["less"] = less
            sa = min(AS, gx)
            if sa:
                nc.scalar.activation(out=th[:, 0:sa], in_=th[:, 0:sa], func=ACT.Copy, scale=-0.5, bias=0.5)
            st[e]["u"], st[e]["th"], st[e]["gx"], st[e]["sa"] = u, th, gx, sa

        def slope_m(e):
            th, gx, sa = st[e]["th"], st[e]["gx"], st[e]["sa"]
            m = ring.tile([P, W], F32, name="slope_sb", bufs=1)
            for c0 in range(0, sa, 512):
                cols = slice(c0, min(c0 + 512, sa))
                nc.gpsimd.tensor_tensor(out=m[:, cols], in0=st[e]["less"][:, cols], in1=th[:, cols], op=ALU.mult)
            for c0 in range(sa, W, GP):
                cols = slice(c0, min(c0 + GP, W))
                nc.gpsimd.tensor_scalar(out=m[:, cols], in0=th[:, cols], scalar1=-0.5, scalar2=0.5, op0=ALU.mult, op1=ALU.add)
            for c0 in range(sa, gx, 512):
                cols = slice(c0, min(c0 + 512, gx))
                nc.gpsimd.tensor_tensor(out=m[:, cols], in0=st[e]["less"][:, cols], in1=m[:, cols], op=ALU.mult)
            st[e]["m"] = m

        def slope_x(e):
            gx = st[e]["gx"]
            step = (W - gx) // 1
            for c0 in range(gx, W, step):
                uf = st[e]["u"][:, c0:c0 + step]
                mf = st[e]["m"][:, c0:c0 + step]
                nc.vector.scalar_tensor_tensor(out=mf, in0=uf, scalar=-1.0, in1=mf, op0=ALU.add, op1=ALU.mult)

        def slope_y(e):
            y = ring.tile([P, W], F32, name="factor_sb", bufs=2)
            b = st[e]["a3"][:].rearrange("p t c -> p (t c)")
            step = W // 1
            for c0 in range(0, W, step):
                cols = slice(c0, c0 + step)
                nc.vector.scalar_tensor_tensor(out=y[:, cols], in0=st[e]["m"][:, cols], scalar=1.0, in1=b[:, cols], op0=ALU.add, op1=ALU.mult)
            st[e]["y"] = y

        def first_product(e):
            codes, scales = st[e]["w2q"]
            banks = []
            for b in range(BLOCKS):
                cols = slice(b * P, (b + 1) * P)
                acc = psum.tile([P, H], F32, name="dh_t_ps", bufs=4 - 1)
                nc.tensor.matmul_mx(
                    out=acc[:], lhsT=st[e]["gw"][:, cols].bitcast(E5M2), lhsT_scale=st[e]["gs"][:, cols],
                    rhs=codes[:].bitcast(E4M3), rhs_scale=scales[:], start=True, stop=True,
                )
                dh_t = ring.tile([P, PACK, P], F32, name="dh_t", bufs=8)
                g = e * BLOCKS + b
                nc.scalar.activation(
                    out=dh_t[:], in_=acc[:].rearrange("p (m t) -> p t m", t=PACK), func=ACT.Copy, scale=gate_cols[:, g:g + 1]
                )
                banks.append(dh_t)
            st[e]["dh_t"] = banks

        def turn(e):
            banks = []
            for b in range(BLOCKS):
                dh = psum.tile([P, PACK, P], F32, name="dh_ps", bufs=4)
                for t in range(PACK):
                    nc.tensor.transpose(dh[:, t, :], st[e]["dh_t"][b][:, t, :], ident[:])
                banks.append(dh)
            st[e]["dh"] = banks

        def products(e):
            da3 = ring.tile([P, C, PACK], BF16, name="da3_bf", bufs=2, align_bytes=64)
            da1 = ring.tile([P, C, PACK], BF16, name="da1_bf", bufs=2, align_bytes=64)
            for b in range(BLOCKS):
                cols = slice(b * P, (b + 1) * P)
                dh = st[e]["dh"][b][:].rearrange("p t (c i) -> p c t i", i=2)
                for da, f in ((da3, st[e]["u"]), (da1, st[e]["y"])):
                    nc.vector.tensor_tensor(
                        out=da[:, cols, :].rearrange("p (c i) t -> p c t i", i=2),
                        in0=dh,
                        in1=f[:].rearrange("p (t c) -> p t c", t=PACK)[:, :, cols].rearrange("p t (c i) -> p c t i", i=2),
                        op=ALU.mult,
                    )
            st[e]["da"] = (da1, da3)

        def second_product(e):
            qs = []
            for m in (1, 0):
                codes = ring.tile([P, C], U32, name="da_codes", bufs=4, align_bytes=64)
                scales = ring.tile([P, C], U8, name="da_scales", bufs=4, align_bytes=64)
                nc.vector.quantize_mx(out=codes[:].bitcast(E5M2), scales=scales[:], in_=st[e]["da"][m][:].rearrange("p c t -> p (c t)"))
                qs.append((m, codes, scales))
            wc, ws = st[e]["w13q"]
            acc = psum.tile([P, C], F32, name="dx_ps", bufs=1)
            for n, (m, codes, scales) in enumerate(qs):
                cols = slice(m * K, (m + 1) * K)
                nc.tensor.matmul_mx(
                    out=acc[:], lhsT=wc[:, cols].bitcast(E4M3), lhsT_scale=ws[:, cols],
                    rhs=codes[:].bitcast(E5M2), rhs_scale=scales[:], start=(n == 0), stop=(n == 1),
                )
            st[e]["dx"] = acc

        def keep_dx(e):
            nc.scalar.copy(out=dx[:, e * C:(e + 1) * C], in_=st[e]["dx"][:])

        nc.gpsimd.memset(dys[:].bitcast(I32), 0)
        nc.gpsimd.memset(gate_rows[32:64, :], 0.0)
        nc.gpsimd.memset(gate_rows[64:128, :], 0.0)
        make_identity(nc, ident[:])

        def load_offs():
            nc.sync.dma_start(offs_sb[:], offs)

        def load_dy():
            nc.sync.dma_start(out=dyw[:], in_=dy_words[0].rearrange("p n t -> p (n t)").bitcast(I32))

        def load_sc():
            for q in range(4):
                nc.sync.dma_start(out=dys[32 * q:32 * q + 4, :].bitcast(I32), in_=dy_scales[0, 4 * q:4 * q + 4, :].bitcast(I32))

        def load_gate():
            nc.sync.dma_start(out=gate_rows[0:32, :], in_=gate[0].rearrange("(b p) -> b p", p=P))

        load_offs()
        load_gate()
        load_sc()
        load_a1(0)
        load_dy()
        load_w2(0)
        load_a1(1)
        load_a3(0)
        load_w13(0)

        gate_ps = psum.tile([P, PACK, P], F32, name="dh_ps", bufs=4)
        nc.tensor.transpose(gate_ps[:, 0, :], gate_rows[:], ident[:])
        nc.scalar.copy(out=gate_cols[:], in_=gate_ps[:, 0, 0:SLOTS // P])

        def loads(e):
            if "a1" not in st[e]:
                load_a1(e)
            load_w2(e)
            if 1 and e + 1 < E:
                load_a1(e + 1)
            load_a3(e)
            load_w13(e)

        gathers(0)
        activations(0)
        cast_w2(0)
        quant_w2(0)
        first_product(0)
        loads(1)
        gathers(1)
        activations(1)
        cast_w2(1)
        cast_w13(0)
        if not 0:
            quant_w2(1)
            quant_w13(0)
        nc.sync.dma_start(pos1_sb[:], pos1)
        nc.sync.dma_start(pos2_sb[:], pos2)
        for e in range(E):
            if e + 2 < E:
                loads(e + 2)
            slope_m(e)
            slope_x(e)
            slope_y(e)
            turn(e)
            if e + 1 < E and not 0:
                first_product(e + 1)
            if 0 and e + 2 < E:
                activations(e + 2)
            if e + 2 < E:
                cast_w2(e + 2)
            if e + 1 < E:
                cast_w13(e + 1)
            if not 0 and e + 2 < E:
                activations(e + 2)
            if e > 0:
                keep_dx(e - 1)
            products(e)
            if 0:
                if e + 1 < E:
                    quant_w2(e + 1)
                    first_product(e + 1)
                quant_w13(e)
            if e + 2 < E:
                gathers(e + 2)
            second_product(e)
            if not 0:
                if e + 2 < E:
                    quant_w2(e + 2)
                if e + 1 < E:
                    quant_w13(e + 1)
        keep_dx(E - 1)

        firsts = []
        for c0 in range(0, T, OUT_PIECE):
            first = ring.tile([P, OUT_PIECE], F32, name="first", tag="dh_t", bufs=8)
            cols = slice(c0 // LIST_ROWS, (c0 + OUT_PIECE) // LIST_ROWS)
            nc.vector.tensor_copy(out=first[:], in_=dx[:].indirect(pos1_sb[:, cols]))
            firsts.append(first)
        c0 = 0
        for width in (512, 512, 512, 384, 128):
            both = ring.tile([P, width], F32, name="both", tag="dh_t", bufs=8)
            cols = slice(c0 // LIST_ROWS, (c0 + width) // LIST_ROWS)
            local = c0 % OUT_PIECE
            nc.vector.tensor_tensor(
                out=both[:], in0=dx[:].indirect(pos2_sb[:, cols]), in1=firsts[c0 // OUT_PIECE][:, local:local + width], op=ALU.add
            )
            nc.sync.dma_start(out=out[:, c0:c0 + width], in_=both[:])
            c0 = c0 + width
